import numpy as np
import ml_dtypes


def mxq(x, axis, fmt="e4m3"):
    dtype, down = {"e4m3": (ml_dtypes.float8_e4m3fn, 7), "e5m2": (ml_dtypes.float8_e5m2, 14)}[fmt]
    v = np.moveaxis(np.asarray(x, np.float32).astype(ml_dtypes.bfloat16).astype(np.float64), axis, -1)
    blocks = v.reshape(v.shape[:-1] + (-1, 32))
    amax = np.abs(blocks).max(-1, keepdims=True)
    byte = np.maximum(np.where(amax > 0, np.frexp(amax)[1] - 1 + 127, 0) - down, 1)
    scale = np.exp2(byte - 127.0)
    codes = (blocks / scale).astype(np.float32).astype(dtype).astype(np.float64)
    return np.moveaxis((codes * scale).reshape(v.shape), -1, axis)


WIDE = False


def mx_kscale(k):
    if not WIDE:
        return np.ones(k)
    levels = np.array([10, -10, 5, -5, 0])
    if k % 512:
        return np.exp2(np.random.permutation(np.resize(levels, k // 32))).repeat(32)
    a = np.empty((k // 512, 16))
    for p in range(k // 512):
        a[p, :8] = np.random.permutation(np.resize(levels, 8))
        for g in range(8):
            far = levels[np.abs(levels - a[p, g]) >= 10]
            a[p, g + 8] = far[np.random.randint(len(far))]
    return np.exp2(a.ravel()).repeat(32)


def f64(x):
    return np.asarray(x).astype(np.float64)


def striped8(idx):
    return np.asarray(idx).reshape(8, -1, 16).transpose(0, 2, 1).reshape(128, -1).astype(np.uint16)


def unstriped8(offs):
    return offs.reshape(8, 16, -1).transpose(0, 2, 1).reshape(8, -1).astype(np.int64)


def pick8(x, idx, run):
    r = np.arange(len(x))
    return x[r[:, None], idx[r % (8 * run) // run]]


E2M1 = np.array([0.0, 0.5, 1.0, 1.5, 2.0, 3.0, 4.0, 6.0, -0.0, -0.5, -1.0, -1.5, -2.0, -3.0, -4.0, -6.0])


def pack_weight(w, fmt):
    k, n = w.shape
    w = f64(np.asarray(w, np.float32).astype(ml_dtypes.bfloat16)).reshape(k // 32, 32, n)
    amax = np.abs(w).max(1)
    if fmt == "e4m3":
        byte = np.frexp(amax)[1] - 1 + 127 - 7
    else:
        mant, ex = np.frexp(amax / 6.0)
        byte = np.where(mant > 0.5, ex, ex - 1) + 127
    byte = np.clip(np.where(amax > 0, byte, 1), 1, 254)
    scaled = (w * np.exp2(127.0 - byte)[:, None, :]).reshape(k, n).astype(np.float32)
    by_word = np.ascontiguousarray(scaled.reshape(k // 512, 128, 4, n).transpose(0, 1, 3, 2))
    if fmt == "e4m3":
        words = by_word.astype(ml_dtypes.float8_e4m3fn).view(np.uint8)
    else:
        c = by_word.astype(ml_dtypes.float4_e2m1fn).view(np.uint8) & 0xF
        words = (c[..., 0::2] | (c[..., 1::2] << 4)).reshape(k // 512, 128, 2 * n)
    return np.ascontiguousarray(words), np.ascontiguousarray(byte.astype(np.uint8).reshape(k // 512, 16, n))


def unpack_weight(words, scales, fmt):
    g, _, n = scales.shape
    words = np.ascontiguousarray(words).reshape(g, 128, n, -1)
    if fmt == "e4m3":
        vals = words.view(ml_dtypes.float8_e4m3fn).astype(np.float64)
    else:
        nib = np.empty((g, 128, n, 4), np.uint8)
        nib[..., 0::2] = words & 0xF
        nib[..., 1::2] = words >> 4
        vals = E2M1[nib]
    vals = vals * np.repeat(np.exp2(scales.astype(np.float64) - 127.0), 8, axis=1)[..., None]
    return vals.transpose(0, 1, 3, 2).reshape(g * 512, n)


D, K, T, U, I, J, Q = 512, 512, 1024, 1024, 512, 256, 128


def setup_inputs():
    n = np.random.standard_normal
    idx = np.stack([np.random.permutation(T)[:I] for _ in range(8)])
    idx2 = np.stack([np.random.permutation(U)[:I] for _ in range(8)])
    idx3 = np.stack([np.random.permutation(T)[:J] for _ in range(8)])
    idx4 = np.stack([np.random.permutation(U)[:J] for _ in range(8)])
    idx5 = np.stack([np.random.permutation(U)[:I] for _ in range(8)])
    fd = mx_kscale(D)
    fk = mx_kscale(K)
    wqp = pack_weight(n((D, K)) * 1.0 / np.sqrt(D) * fd[:, None] * fk, "e4m3")
    cachep = pack_weight(n((K, T)) * 1.0 / np.sqrt(K) / fk[:, None], "e2m1")
    draftp = pack_weight(n((D, U)) * 1.0 / np.sqrt(D) * fd[:, None], "e4m3")
    return {
        "states": (n((D, Q)) * 0.95 / fd[:, None]).astype(np.float32),
        "wq_words": wqp[0],
        "wq_scales": wqp[1],
        "cache_words": cachep[0],
        "cache_scales": cachep[1],
        "draft_words": draftp[0],
        "draft_scales": draftp[1],
        "offs": striped8(idx),
        "offs2": striped8(idx2),
        "offs3": striped8(idx3),
        "offs4": striped8(idx4),
        "offs5": striped8(idx5),
    }


def reference(states, wq_words, wq_scales, cache_words, cache_scales, draft_words, draft_scales, offs, offs2, offs3, offs4, offs5):
    idx = unstriped8(offs)
    idx2 = unstriped8(offs2)
    idx3 = unstriped8(offs3)
    idx4 = unstriped8(offs4)
    idx5 = unstriped8(offs5)
    wqu = unpack_weight(wq_words, wq_scales, "e4m3")
    cacheu = unpack_weight(cache_words, cache_scales, "e2m1")
    draftu = unpack_weight(draft_words, draft_scales, "e4m3")
    statesq = mxq(f64(states), 0, "e4m3")
    qv = wqu.T @ statesq
    qvq = mxq(qv, 0, "e4m3")
    a = qvq.T @ cacheu
    b = statesq.T @ draftu
    w = pick8(a, idx, 16) - pick8(b, idx2, 16)
    acc = w[:, 0:0 + J]
    rej = w[:, 256:256 + J]
    f1 = np.zeros((Q, T))
    f1[np.arange(Q)[:, None], idx3[np.arange(Q) % 128 // 16]] = acc
    f2 = np.zeros((Q, U))
    f2[np.arange(Q)[:, None], idx4[np.arange(Q) % 128 // 16]] = rej
    aa = a + f1
    bb = b - f2
    y = np.maximum(pick8(aa, idx, 16), pick8(bb, idx5, 16))
    return y

@@ -1,0 +1,149 @@
+from contextlib import ExitStack
+
+import concourse.mybir as mybir
+
+D, K, T, U, I, J, Q = 512, 512, 1024, 1024, 512, 256, 128
+FLOPS = 2 * D * K * Q + 2 * K * Q * T + 2 * D * Q * U
+
+F32 = mybir.dt.float32
+BF16 = mybir.dt.bfloat16
+I32 = mybir.dt.int32
+U32 = mybir.dt.uint32
+U16 = mybir.dt.uint16
+U8 = mybir.dt.uint8
+FP8X4 = mybir.dt.float8_e4m3fn_x4
+FP4X4 = mybir.dt.float4_e2m1fn_x4
+ALU = mybir.AluOpType
+COPY = mybir.ActivationFunctionType.Copy
+
+P = 128
+PACK = 4
+
+
+def load_scale_rows(queue, stage, scales):
+    rows = scales[0].bitcast(I32).rearrange("(h g r) w -> g r h w", h=2, g=2)
+    words = stage[:].rearrange("p h c -> p (h c)").bitcast(I32).rearrange("p (h w) -> p h w", h=2)
+    for g in range(2):
+        queue.dma_start(out=words[32 * g : 32 * g + 4, :, :], in_=rows[g])
+
+
+def spread_scale_rows(nc, stage):
+    nc.vector.tensor_copy(out=stage[64:128, 0, :].bitcast(I32), in_=stage[0:64, 1, :].bitcast(I32))
+
+
+def tile_attend_acceptback_side_kernel(
+    tc, states, wq_words, wq_scales, cache_words, cache_scales, draft_words, draft_scales,
+    offs, offs2, offs3, offs4, offs5, out,
+):
+    nc = tc.nc
+    with ExitStack() as ctx:
+        sb = ctx.enter_context(tc.tile_pool(name="sb", bufs=1))
+        ps = ctx.enter_context(tc.psum_pool(name="ps", bufs=1))
+
+        wq_plane = sb.tile([P, 2, K], U8, align_bytes=64)
+        draft_plane = sb.tile([P, 2, U], U8, align_bytes=64)
+        cache_plane = sb.tile([P, T], U8, align_bytes=64)
+        f1 = sb.tile([P, T], F32)
+        for plane in (wq_plane, draft_plane):
+            nc.vector.memset(plane[0:64].rearrange("p h c -> p (h c)").bitcast(I32), 0)
+        nc.vector.memset(cache_plane[:].bitcast(I32), 0)
+        nc.vector.memset(f1[:], 0.0)
+
+        raw = sb.tile([P, PACK, Q], F32)
+        wq_raw = sb.tile([P, K], U32, align_bytes=64)
+        draft_w = sb.tile([P, U], U32, align_bytes=64)
+        cache_w = sb.tile([P, 2 * T], U8, align_bytes=64)
+        l1 = sb.tile([P, I // 16], U16)
+        l2 = sb.tile([P, I // 16], U16)
+        l3 = sb.tile([P, J // 16], U16)
+        l4 = sb.tile([P, J // 16], U16)
+        l5 = sb.tile([P, I // 16], U16)
+
+        nc.sync.dma_start(out=raw[:], in_=states.rearrange("(p j) q -> p j q", j=PACK))
+        load_scale_rows(nc.sync, wq_plane, wq_scales)
+        nc.sync.dma_start(out=wq_raw[:].bitcast(I32), in_=wq_words[0].rearrange("p n t -> p (n t)").bitcast(I32))
+        load_scale_rows(nc.sync, draft_plane, draft_scales)
+        nc.sync.dma_start(out=draft_w[:].bitcast(I32), in_=draft_words[0].rearrange("p n t -> p (n t)").bitcast(I32))
+        nc.sync.dma_start(out=cache_w[:].bitcast(I32), in_=cache_words[0].bitcast(I32))
+        for g in range(4):
+            nc.sync.dma_start(out=cache_plane[32 * g : 32 * g + 4, :].bitcast(I32), in_=cache_scales[0, 4 * g : 4 * g + 4, :].bitcast(I32))
+        nc.sync.dma_start(l2[:], offs2)
+        nc.sync.dma_start(l1[:], offs)
+        nc.sync.dma_start(l3[:], offs3)
+        nc.sync.dma_start(l4[:], offs4)
+        nc.sync.dma_start(l5[:], offs5)
+
+        spread_scale_rows(nc, wq_plane)
+        st_b = sb.tile([P, Q, PACK], BF16, align_bytes=64)
+        nc.vector.tensor_copy(out=st_b[:], in_=raw[:].rearrange("p j q -> p q j"))
+        wq_s = sb.tile([P, K], U8, align_bytes=64)
+        nc.vector.tensor_copy(out=wq_s[:].rearrange("p (t m) -> p t m", t=PACK), in_=wq_plane[:, 0, :].rearrange("p (m t) -> p t m", t=PACK))
+        wq_w = sb.tile([P, K], U32, align_bytes=64)
+        nc.scalar.copy(out=wq_w[:].rearrange("p (t m) -> p t m", t=PACK), in_=wq_raw[:].rearrange("p (m t) -> p t m", t=PACK))
+
+        st_w = sb.tile([P, Q], U32, align_bytes=64)
+        st_s = sb.tile([P, Q], U8, align_bytes=64)
+        nc.vector.quantize_mx(out=st_w[:].bitcast(FP8X4), scales=st_s[:], in_=st_b[:].rearrange("p q j -> p (q j)"))
+        spread_scale_rows(nc, draft_plane)
+
+        qv_ps = ps.tile([P, PACK, Q], F32)
+        for t in range(PACK):
+            cols = slice(P * t, P * (t + 1))
+            nc.tensor.matmul_mx(out=qv_ps[:, t, :], lhsT=wq_w[:, cols].bitcast(FP8X4), lhsT_scale=wq_s[:, cols],
+                                rhs=st_w[:].bitcast(FP8X4), rhs_scale=st_s[:], start=True, stop=True)
+        b_ps = [ps.tile([P, 512], F32, name="b_ps%d" % n) for n in range(2)]
+        for n in range(2):
+            cols = slice(512 * n, 512 * (n + 1))
+            nc.tensor.matmul_mx(out=b_ps[n][:], lhsT=st_w[:].bitcast(FP8X4), lhsT_scale=st_s[:],
+                                rhs=draft_w[:, cols].bitcast(FP8X4), rhs_scale=draft_plane[:, 0, cols], start=True, stop=True)
+
+        qv_b = sb.tile([P, Q, PACK], BF16, align_bytes=64, tag="qv_b_then_f2")
+        nc.vector.tensor_copy(out=qv_b[:], in_=qv_ps[:].rearrange("p t q -> p q t"))
+        qv_w = sb.tile([P, Q], U32, align_bytes=64)
+        qv_s = sb.tile([P, Q], U8, align_bytes=64)
+        nc.vector.quantize_mx(out=qv_w[:].bitcast(FP8X4), scales=qv_s[:], in_=qv_b[:].rearrange("p q j -> p (q j)"))
+
+        f2 = sb.tile([P, U], F32, align_bytes=64, tag="qv_b_then_f2")
+        nc.gpsimd.memset(f2[:], 0.0)
+
+        b_sb = sb.tile([P, U], F32)
+        nc.scalar.copy(out=b_sb[:, 0:512], in_=b_ps[0][:])
+        nc.scalar.copy(out=b_sb[:, 512:1024], in_=b_ps[1][:])
+        gb = [sb.tile([P, J], F32, name="gb%d" % h) for h in range(2)]
+        nc.scalar.activation(gb[0][:], b_sb[:].indirect(l2[:, 0:16]), COPY)
+
+        a_ps = [ps.tile([P, 256], F32, name="a_ps%d" % n) for n in range(4)]
+        a_sb = sb.tile([P, T], F32)
+        for n in range(4):
+            nc.tensor.matmul_mx(out=a_ps[n][:], lhsT=qv_w[:].bitcast(FP8X4), lhsT_scale=qv_s[:],
+                                rhs=cache_w[:, 512 * n : 512 * (n + 1)].bitcast(FP4X4),
+                                rhs_scale=cache_plane[:, 256 * n : 256 * (n + 1)], start=True, stop=True)
+        for n in range(4):
+            cols = slice(256 * n, 256 * (n + 1))
+            if n < 3:
+                nc.vector.tensor_copy(out=a_sb[:, cols], in_=a_ps[n][:])
+            else:
+                nc.scalar.copy(out=a_sb[:, cols], in_=a_ps[n][:])
+
+        acc = sb.tile([P, J], F32)
+        rej = sb.tile([P, J], F32)
+        nc.vector.tensor_tensor(acc[:], a_sb[:].indirect(l1[:, 0:16]), gb[0][:], ALU.subtract)
+        nc.scalar.activation(f1[:].indirect(l3[:]), acc[:], COPY)
+        nc.vector.tensor_copy(gb[1][:], b_sb[:].indirect(l2[:, 16:32]))
+        nc.vector.tensor_tensor(rej[:], a_sb[:].indirect(l1[:, 16:32]), gb[1][:], ALU.subtract)
+        nc.scalar.activation(f2[:].indirect(l4[:]), rej[:], COPY)
+
+        aa = sb.tile([P, T], F32)
+        nc.vector.tensor_tensor(aa[:], a_sb[:], f1[:], ALU.add)
+        gaa = sb.tile([P, I], F32)
+        nc.scalar.activation(gaa[:], aa[:].indirect(l1[:]), COPY)
+        bb = sb.tile([P, U], F32)
+        nc.vector.tensor_tensor(bb[:], b_sb[:], f2[:], ALU.subtract)
+        gbb = [sb.tile([P, J], F32, name="gbb%d" % h) for h in range(2)]
+        nc.vector.tensor_copy(gbb[0][:], bb[:].indirect(l5[:, 0:16]))
+        nc.scalar.activation(gbb[1][:], bb[:].indirect(l5[:, 16:32]), COPY)
+        for h, queue in enumerate((nc.sync, nc.scalar)):
+            cols = slice(J * h, J * (h + 1))
+            res = sb.tile([P, J], F32, name="res%d" % h)
+            nc.vector.tensor_tensor(res[:], gaa[:, cols], gbb[h][:], ALU.max)
+            queue.dma_start(out=out[:, cols], in_=res[:])

@@ -50,7 +50,7 @@ def tile_attend_acceptback_side_kernel(
         nc.vector.memset(f1[:], 0.0)
 
         raw = sb.tile([P, PACK, Q], F32)
-        wq_raw = sb.tile([P, K], U32, align_bytes=64)
+        wq_raw = [sb.tile([P, K // 2], U32, align_bytes=64, name="wq_raw%d" % h) for h in range(2)]
         draft_w = sb.tile([P, U], U32, align_bytes=64)
         cache_w = sb.tile([P, 2 * T], U8, align_bytes=64)
         l1 = sb.tile([P, I // 16], U16)
@@ -60,8 +60,9 @@ def tile_attend_acceptback_side_kernel(
         l5 = sb.tile([P, I // 16], U16)
 
         nc.sync.dma_start(out=raw[:], in_=states.rearrange("(p j) q -> p j q", j=PACK))
-        load_scale_rows(nc.sync, wq_plane, wq_scales)
-        nc.sync.dma_start(out=wq_raw[:].bitcast(I32), in_=wq_words[0].rearrange("p n t -> p (n t)").bitcast(I32))
+        load_scale_rows(nc.scalar, wq_plane, wq_scales)
+        for h in range(2):
+            nc.sync.dma_start(out=wq_raw[h][:].bitcast(I32), in_=wq_words[0, :, 256 * h : 256 * (h + 1), :].rearrange("p n t -> p (n t)").bitcast(I32))
         load_scale_rows(nc.sync, draft_plane, draft_scales)
         nc.sync.dma_start(out=draft_w[:].bitcast(I32), in_=draft_words[0].rearrange("p n t -> p (n t)").bitcast(I32))
         nc.sync.dma_start(out=cache_w[:].bitcast(I32), in_=cache_words[0].bitcast(I32))
@@ -77,23 +78,27 @@ def tile_attend_acceptback_side_kernel(
         st_b = sb.tile([P, Q, PACK], BF16, align_bytes=64)
         nc.vector.tensor_copy(out=st_b[:], in_=raw[:].rearrange("p j q -> p q j"))
         wq_s = sb.tile([P, K], U8, align_bytes=64)
-        nc.vector.tensor_copy(out=wq_s[:].rearrange("p (t m) -> p t m", t=PACK), in_=wq_plane[:, 0, :].rearrange("p (m t) -> p t m", t=PACK))
+        wq_s_in = wq_plane[:, 0, :].rearrange("p (m t) -> p t m", t=PACK)
+        nc.vector.tensor_copy(out=wq_s[:, 0:P], in_=wq_s_in[:, 0, :])
         wq_w = sb.tile([P, K], U32, align_bytes=64)
-        nc.scalar.copy(out=wq_w[:].rearrange("p (t m) -> p t m", t=PACK), in_=wq_raw[:].rearrange("p (m t) -> p t m", t=PACK))
+        for h in range(2):
+            nc.scalar.copy(out=wq_w[:].rearrange("p (t m) -> p m t", t=PACK)[:, 64 * h : 64 * (h + 1), :], in_=wq_raw[h][:].rearrange("p (m t) -> p m t", t=PACK))
 
         st_w = sb.tile([P, Q], U32, align_bytes=64)
         st_s = sb.tile([P, Q], U8, align_bytes=64)
         nc.vector.quantize_mx(out=st_w[:].bitcast(FP8X4), scales=st_s[:], in_=st_b[:].rearrange("p q j -> p (q j)"))
+        for t in range(1, PACK):
+            nc.vector.tensor_copy(out=wq_s[:, P * t : P * (t + 1)], in_=wq_s_in[:, t, :])
         spread_scale_rows(nc, draft_plane)
 
-        qv_ps = ps.tile([P, PACK, Q], F32)
+        qv_ps = ps.tile([P, PACK, Q], F32, tag="qv_then_a0")
         for t in range(PACK):
             cols = slice(P * t, P * (t + 1))
             nc.tensor.matmul_mx(out=qv_ps[:, t, :], lhsT=wq_w[:, cols].bitcast(FP8X4), lhsT_scale=wq_s[:, cols],
                                 rhs=st_w[:].bitcast(FP8X4), rhs_scale=st_s[:], start=True, stop=True)
-        b_ps = [ps.tile([P, 512], F32, name="b_ps%d" % n) for n in range(2)]
-        for n in range(2):
-            cols = slice(512 * n, 512 * (n + 1))
+        b_ps = [ps.tile([P, 256], F32, name="b_ps%d" % n) for n in range(4)]
+        for n in range(4):
+            cols = slice(256 * n, 256 * (n + 1))
             nc.tensor.matmul_mx(out=b_ps[n][:], lhsT=st_w[:].bitcast(FP8X4), lhsT_scale=st_s[:],
                                 rhs=draft_w[:, cols].bitcast(FP8X4), rhs_scale=draft_plane[:, 0, cols], start=True, stop=True)
 
@@ -107,12 +112,13 @@ def tile_attend_acceptback_side_kernel(
         nc.gpsimd.memset(f2[:], 0.0)
 
         b_sb = sb.tile([P, U], F32)
-        nc.scalar.copy(out=b_sb[:, 0:512], in_=b_ps[0][:])
-        nc.scalar.copy(out=b_sb[:, 512:1024], in_=b_ps[1][:])
+        for n in range(4):
+            cols = slice(256 * n, 256 * (n + 1))
+            nc.scalar.copy(out=b_sb[:, cols], in_=b_ps[n][:])
         gb = [sb.tile([P, J], F32, name="gb%d" % h) for h in range(2)]
         nc.scalar.activation(gb[0][:], b_sb[:].indirect(l2[:, 0:16]), COPY)
 
-        a_ps = [ps.tile([P, 256], F32, name="a_ps%d" % n) for n in range(4)]
+        a_ps = [ps.tile([P, 256], F32, name="a_ps%d" % n, tag="qv_then_a0" if n == 0 else "a_ps%d" % n) for n in range(4)]
         a_sb = sb.tile([P, T], F32)
         for n in range(4):
             nc.tensor.matmul_mx(out=a_ps[n][:], lhsT=qv_w[:].bitcast(FP8X4), lhsT_scale=qv_s[:],
@@ -125,11 +131,11 @@ def tile_attend_acceptback_side_kernel(
             else:
                 nc.scalar.copy(out=a_sb[:, cols], in_=a_ps[n][:])
 
+        nc.scalar.activation(gb[1][:], b_sb[:].indirect(l2[:, 16:32]), COPY)
         acc = sb.tile([P, J], F32)
         rej = sb.tile([P, J], F32)
         nc.vector.tensor_tensor(acc[:], a_sb[:].indirect(l1[:, 0:16]), gb[0][:], ALU.subtract)
         nc.scalar.activation(f1[:].indirect(l3[:]), acc[:], COPY)
-        nc.vector.tensor_copy(gb[1][:], b_sb[:].indirect(l2[:, 16:32]))
         nc.vector.tensor_tensor(rej[:], a_sb[:].indirect(l1[:, 16:32]), gb[1][:], ALU.subtract)
         nc.scalar.activation(f2[:].indirect(l4[:]), rej[:], COPY)
 
@@ -139,11 +145,11 @@ def tile_attend_acceptback_side_kernel(
         nc.scalar.activation(gaa[:], aa[:].indirect(l1[:]), COPY)
         bb = sb.tile([P, U], F32)
         nc.vector.tensor_tensor(bb[:], b_sb[:], f2[:], ALU.subtract)
-        gbb = [sb.tile([P, J], F32, name="gbb%d" % h) for h in range(2)]
-        nc.vector.tensor_copy(gbb[0][:], bb[:].indirect(l5[:, 0:16]))
-        nc.scalar.activation(gbb[1][:], bb[:].indirect(l5[:, 16:32]), COPY)
-        for h, queue in enumerate((nc.sync, nc.scalar)):
-            cols = slice(J * h, J * (h + 1))
-            res = sb.tile([P, J], F32, name="res%d" % h)
-            nc.vector.tensor_tensor(res[:], gaa[:, cols], gbb[h][:], ALU.max)
-            queue.dma_start(out=out[:, cols], in_=res[:])
+        gbb = sb.tile([P, I], F32)
+        nc.vector.tensor_copy(gbb[:, 0:J], bb[:].indirect(l5[:, 0:16]))
+        nc.scalar.activation(gbb[:, J:I], bb[:].indirect(l5[:, 16:32]), COPY)
+        res = sb.tile([P, J], F32)
+        nc.vector.tensor_tensor(res[:], gaa[:, J:I], gbb[:, J:I], ALU.max)
+        nc.scalar.dma_start(out=out[:, J:I], in_=res[:])
+        nc.vector.tensor_tensor(gbb[:, J:I], gaa[:, 0:J], gbb[:, 0:J], ALU.max)
+        nc.sync.dma_start(out=out[:, 0:J], in_=gbb[:, J:I])

@@ -20,15 +20,12 @@ P = 128
 PACK = 4
 
 
-def load_scale_rows(queue, stage, scales):
-    rows = scales[0].bitcast(I32).rearrange("(h g r) w -> g r h w", h=2, g=2)
+def load_scale_rows(queue, stage, scales, first, apart):
+    order = "(h g r) w -> g r h w" if apart == 32 else "(g h r) w -> g r h w"
+    rows = scales[0].bitcast(I32).rearrange(order, h=2, g=2)
     words = stage[:].rearrange("p h c -> p (h c)").bitcast(I32).rearrange("p (h w) -> p h w", h=2)
     for g in range(2):
-        queue.dma_start(out=words[32 * g : 32 * g + 4, :, :], in_=rows[g])
-
-
-def spread_scale_rows(nc, stage):
-    nc.vector.tensor_copy(out=stage[64:128, 0, :].bitcast(I32), in_=stage[0:64, 1, :].bitcast(I32))
+        queue.dma_start(out=words[apart * g + first : apart * g + first + 4, :, :], in_=rows[g])
 
 
 def tile_attend_acceptback_side_kernel(
@@ -44,8 +41,8 @@ def tile_attend_acceptback_side_kernel(
         draft_plane = sb.tile([P, 2, U], U8, align_bytes=64)
         cache_plane = sb.tile([P, T], U8, align_bytes=64)
         f1 = sb.tile([P, T], F32)
-        for plane in (wq_plane, draft_plane):
-            nc.vector.memset(plane[0:64].rearrange("p h c -> p (h c)").bitcast(I32), 0)
+        nc.vector.memset(wq_plane[0:64].rearrange("p h c -> p (h c)").bitcast(I32), 0)
+        nc.vector.memset(draft_plane[:].rearrange("p h c -> p (h c)").bitcast(I32), 0)
         nc.vector.memset(cache_plane[:].bitcast(I32), 0)
         nc.vector.memset(f1[:], 0.0)
 
@@ -60,10 +57,10 @@ def tile_attend_acceptback_side_kernel(
         l5 = sb.tile([P, I // 16], U16)
 
         nc.sync.dma_start(out=raw[:], in_=states.rearrange("(p j) q -> p j q", j=PACK))
-        load_scale_rows(nc.scalar, wq_plane, wq_scales)
+        load_scale_rows(nc.scalar, wq_plane, wq_scales, 4, 32)
         for h in range(2):
             nc.sync.dma_start(out=wq_raw[h][:].bitcast(I32), in_=wq_words[0, :, 256 * h : 256 * (h + 1), :].rearrange("p n t -> p (n t)").bitcast(I32))
-        load_scale_rows(nc.sync, draft_plane, draft_scales)
+        load_scale_rows(nc.sync, draft_plane, draft_scales, 8, 64)
         nc.sync.dma_start(out=draft_w[:].bitcast(I32), in_=draft_words[0].rearrange("p n t -> p (n t)").bitcast(I32))
         nc.sync.dma_start(out=cache_w[:].bitcast(I32), in_=cache_words[0].bitcast(I32))
         for g in range(4):
@@ -74,7 +71,7 @@ def tile_attend_acceptback_side_kernel(
         nc.sync.dma_start(l4[:], offs4)
         nc.sync.dma_start(l5[:], offs5)
 
-        spread_scale_rows(nc, wq_plane)
+        nc.vector.tensor_copy(out=wq_plane[64:128, 0, :].bitcast(I32), in_=wq_plane[0:64, 1, :].bitcast(I32))
         st_b = sb.tile([P, Q, PACK], BF16, align_bytes=64)
         nc.vector.tensor_copy(out=st_b[:], in_=raw[:].rearrange("p j q -> p q j"))
         wq_s = sb.tile([P, K], U8, align_bytes=64)
@@ -89,18 +86,19 @@ def tile_attend_acceptback_side_kernel(
         nc.vector.quantize_mx(out=st_w[:].bitcast(FP8X4), scales=st_s[:], in_=st_b[:].rearrange("p q j -> p (q j)"))
         for t in range(1, PACK):
             nc.vector.tensor_copy(out=wq_s[:, P * t : P * (t + 1)], in_=wq_s_in[:, t, :])
-        spread_scale_rows(nc, draft_plane)
+        for g in range(2):
+            nc.vector.tensor_copy(out=draft_plane[64 * g + 32 : 64 * g + 64, 0, :].bitcast(I32), in_=draft_plane[64 * g : 64 * g + 32, 1, :].bitcast(I32))
 
         qv_ps = ps.tile([P, PACK, Q], F32, tag="qv_then_a0")
         for t in range(PACK):
             cols = slice(P * t, P * (t + 1))
-            nc.tensor.matmul_mx(out=qv_ps[:, t, :], lhsT=wq_w[:, cols].bitcast(FP8X4), lhsT_scale=wq_s[:, cols],
+            nc.tensor.matmul_mx(out=qv_ps[:, t, :], lhsT=wq_w[:, cols].bitcast(FP8X4), lhsT_scale=wq_s[4:128, cols],
                                 rhs=st_w[:].bitcast(FP8X4), rhs_scale=st_s[:], start=True, stop=True)
         b_ps = [ps.tile([P, 256], F32, name="b_ps%d" % n) for n in range(4)]
         for n in range(4):
             cols = slice(256 * n, 256 * (n + 1))
             nc.tensor.matmul_mx(out=b_ps[n][:], lhsT=st_w[:].bitcast(FP8X4), lhsT_scale=st_s[:],
-                                rhs=draft_w[:, cols].bitcast(FP8X4), rhs_scale=draft_plane[:, 0, cols], start=True, stop=True)
+                                rhs=draft_w[:, cols].bitcast(FP8X4), rhs_scale=draft_plane[8:128, 0, cols], start=True, stop=True)
 
         qv_b = sb.tile([P, Q, PACK], BF16, align_bytes=64, tag="qv_b_then_f2")
         nc.vector.tensor_copy(out=qv_b[:], in_=qv_ps[:].rearrange("p t q -> p q t"))

@@ -142,12 +142,15 @@ def tile_attend_acceptback_side_kernel(
         gaa = sb.tile([P, I], F32)
         nc.scalar.activation(gaa[:], aa[:].indirect(l1[:]), COPY)
         bb = sb.tile([P, U], F32)
-        nc.vector.tensor_tensor(bb[:], b_sb[:], f2[:], ALU.subtract)
+        for n in range(3):
+            cols = slice(256 * n, 256 * (n + 1))
+            nc.vector.tensor_tensor(bb[:, cols], b_ps[n][:], f2[:, cols], ALU.subtract)
+        nc.gpsimd.tensor_tensor(bb[:, 768:U], b_sb[:, 768:U], f2[:, 768:U], ALU.subtract)
         gbb = sb.tile([P, I], F32)
         nc.vector.tensor_copy(gbb[:, 0:J], bb[:].indirect(l5[:, 0:16]))
         nc.scalar.activation(gbb[:, J:I], bb[:].indirect(l5[:, 16:32]), COPY)
-        res = sb.tile([P, J], F32)
-        nc.vector.tensor_tensor(res[:], gaa[:, J:I], gbb[:, J:I], ALU.max)
-        nc.scalar.dma_start(out=out[:, J:I], in_=res[:])
-        nc.vector.tensor_tensor(gbb[:, J:I], gaa[:, 0:J], gbb[:, 0:J], ALU.max)
-        nc.sync.dma_start(out=out[:, 0:J], in_=gbb[:, J:I])
+        for h, queue in enumerate((nc.sync, nc.scalar)):
+            cols = slice(J * h, J * (h + 1))
+            res = sb.tile([P, J], F32, name="res%d" % h)
+            nc.vector.tensor_tensor(res[:], gaa[:, cols], gbb[:, cols], ALU.max)
+            queue.dma_start(out=out[:, cols], in_=res[:])

from contextlib import ExitStack

import concourse.mybir as mybir

D, K, T, U, I, J, Q = 512, 512, 1024, 1024, 512, 256, 128
FLOPS = 2 * D * K * Q + 2 * K * Q * T + 2 * D * Q * U

F32 = mybir.dt.float32
BF16 = mybir.dt.bfloat16
I32 = mybir.dt.int32
U32 = mybir.dt.uint32
U16 = mybir.dt.uint16
U8 = mybir.dt.uint8
FP8X4 = mybir.dt.float8_e4m3fn_x4
FP4X4 = mybir.dt.float4_e2m1fn_x4
ALU = mybir.AluOpType
COPY = mybir.ActivationFunctionType.Copy

P = 128
PACK = 4


def load_scale_rows(queue, stage, scales, first, apart):
    order = "(h g r) w -> g r h w" if apart == 32 else "(g h r) w -> g r h w"
    rows = scales[0].bitcast(I32).rearrange(order, h=2, g=2)
    words = stage[:].rearrange("p h c -> p (h c)").bitcast(I32).rearrange("p (h w) -> p h w", h=2)
    for g in range(2):
        queue.dma_start(out=words[apart * g + first : apart * g + first + 4, :, :], in_=rows[g])


def tile_attend_acceptback_side_kernel(
    tc, states, wq_words, wq_scales, cache_words, cache_scales, draft_words, draft_scales,
    offs, offs2, offs3, offs4, offs5, out,
):
    nc = tc.nc
    with ExitStack() as ctx:
        sb = ctx.enter_context(tc.tile_pool(name="sb", bufs=1))
        ps = ctx.enter_context(tc.psum_pool(name="ps", bufs=1))

        wq_plane = sb.tile([P, 2, K], U8, align_bytes=64)
        draft_plane = sb.tile([P, 2, U], U8, align_bytes=64)
        cache_plane = sb.tile([P, T], U8, align_bytes=64)
        f1 = sb.tile([P, T], F32)
        nc.vector.memset(wq_plane[0:64].rearrange("p h c -> p (h c)").bitcast(I32), 0)
        nc.vector.memset(draft_plane[:].rearrange("p h c -> p (h c)").bitcast(I32), 0)
        nc.vector.memset(cache_plane[:].bitcast(I32), 0)
        nc.vector.memset(f1[:], 0.0)

        raw = sb.tile([P, PACK, Q], F32)
        wq_raw = [sb.tile([P, K // 2], U32, align_bytes=64, name="wq_raw%d" % h) for h in range(2)]
        draft_w = sb.tile([P, U], U32, align_bytes=64)
        cache_w = sb.tile([P, 2 * T], U8, align_bytes=64)
        l1 = sb.tile([P, I // 16], U16)
        l2 = sb.tile([P, I // 16], U16)
        l3 = sb.tile([P, J // 16], U16)
        l4 = sb.tile([P, J // 16], U16)
        l5 = sb.tile([P, I // 16], U16)

        nc.sync.dma_start(out=raw[:], in_=states.rearrange("(p j) q -> p j q", j=PACK))
        load_scale_rows(nc.scalar, wq_plane, wq_scales, 4, 32)
        for h in range(2):
            nc.sync.dma_start(out=wq_raw[h][:].bitcast(I32), in_=wq_words[0, :, 256 * h : 256 * (h + 1), :].rearrange("p n t -> p (n t)").bitcast(I32))
        load_scale_rows(nc.sync, draft_plane, draft_scales, 8, 64)
        nc.sync.dma_start(out=draft_w[:].bitcast(I32), in_=draft_words[0].rearrange("p n t -> p (n t)").bitcast(I32))
        nc.sync.dma_start(out=cache_w[:].bitcast(I32), in_=cache_words[0].bitcast(I32))
        for g in range(4):
            nc.sync.dma_start(out=cache_plane[32 * g : 32 * g + 4, :].bitcast(I32), in_=cache_scales[0, 4 * g : 4 * g + 4, :].bitcast(I32))
        nc.sync.dma_start(l2[:], offs2)
        nc.sync.dma_start(l1[:], offs)
        nc.sync.dma_start(l3[:], offs3)
        nc.sync.dma_start(l4[:], offs4)
        nc.sync.dma_start(l5[:], offs5)

        nc.vector.tensor_copy(out=wq_plane[64:128, 0, :].bitcast(I32), in_=wq_plane[0:64, 1, :].bitcast(I32))
        st_b = sb.tile([P, Q, PACK], BF16, align_bytes=64)
        nc.vector.tensor_copy(out=st_b[:], in_=raw[:].rearrange("p j q -> p q j"))
        wq_s = sb.tile([P, K], U8, align_bytes=64)
        wq_s_in = wq_plane[:, 0, :].rearrange("p (m t) -> p t m", t=PACK)
        nc.vector.tensor_copy(out=wq_s[:, 0:P], in_=wq_s_in[:, 0, :])
        wq_w = sb.tile([P, K], U32, align_bytes=64)
        for h in range(2):
            nc.scalar.copy(out=wq_w[:].rearrange("p (t m) -> p m t", t=PACK)[:, 64 * h : 64 * (h + 1), :], in_=wq_raw[h][:].rearrange("p (m t) -> p m t", t=PACK))

        st_w = sb.tile([P, Q], U32, align_bytes=64)
        st_s = sb.tile([P, Q], U8, align_bytes=64)
        nc.vector.quantize_mx(out=st_w[:].bitcast(FP8X4), scales=st_s[:], in_=st_b[:].rearrange("p q j -> p (q j)"))
        for t in range(1, PACK):
            nc.vector.tensor_copy(out=wq_s[:, P * t : P * (t + 1)], in_=wq_s_in[:, t, :])
        for g in range(2):
            nc.vector.tensor_copy(out=draft_plane[64 * g + 32 : 64 * g + 64, 0, :].bitcast(I32), in_=draft_plane[64 * g : 64 * g + 32, 1, :].bitcast(I32))

        qv_ps = ps.tile([P, PACK, Q], F32, tag="qv_then_a0")
        for t in range(PACK):
            cols = slice(P * t, P * (t + 1))
            nc.tensor.matmul_mx(out=qv_ps[:, t, :], lhsT=wq_w[:, cols].bitcast(FP8X4), lhsT_scale=wq_s[4:128, cols],
                                rhs=st_w[:].bitcast(FP8X4), rhs_scale=st_s[:], start=True, stop=True)
        b_ps = [ps.tile([P, 256], F32, name="b_ps%d" % n) for n in range(4)]
        for n in range(4):
            cols = slice(256 * n, 256 * (n + 1))
            nc.tensor.matmul_mx(out=b_ps[n][:], lhsT=st_w[:].bitcast(FP8X4), lhsT_scale=st_s[:],
                                rhs=draft_w[:, cols].bitcast(FP8X4), rhs_scale=draft_plane[8:128, 0, cols], start=True, stop=True)

        qv_b = sb.tile([P, Q, PACK], BF16, align_bytes=64, tag="qv_b_then_f2")
        nc.vector.tensor_copy(out=qv_b[:], in_=qv_ps[:].rearrange("p t q -> p q t"))
        qv_w = sb.tile([P, Q], U32, align_bytes=64)
        qv_s = sb.tile([P, Q], U8, align_bytes=64)
        nc.vector.quantize_mx(out=qv_w[:].bitcast(FP8X4), scales=qv_s[:], in_=qv_b[:].rearrange("p q j -> p (q j)"))

        f2 = sb.tile([P, U], F32, align_bytes=64, tag="qv_b_then_f2")
        nc.gpsimd.memset(f2[:], 0.0)

        b_sb = sb.tile([P, U], F32)
        for n in range(4):
            cols = slice(256 * n, 256 * (n + 1))
            nc.scalar.copy(out=b_sb[:, cols], in_=b_ps[n][:])
        gb = [sb.tile([P, J], F32, name="gb%d" % h) for h in range(2)]
        nc.scalar.activation(gb[0][:], b_sb[:].indirect(l2[:, 0:16]), COPY)

        a_ps = [ps.tile([P, 256], F32, name="a_ps%d" % n, tag="qv_then_a0" if n == 0 else "a_ps%d" % n) for n in range(4)]
        a_sb = sb.tile([P, T], F32)
        for n in range(4):
            nc.tensor.matmul_mx(out=a_ps[n][:], lhsT=qv_w[:].bitcast(FP8X4), lhsT_scale=qv_s[:],
                                rhs=cache_w[:, 512 * n : 512 * (n + 1)].bitcast(FP4X4),
                                rhs_scale=cache_plane[:, 256 * n : 256 * (n + 1)], start=True, stop=True)
        for n in range(4):
            cols = slice(256 * n, 256 * (n + 1))
            if n < 3:
                nc.vector.tensor_copy(out=a_sb[:, cols], in_=a_ps[n][:])
            else:
                nc.scalar.copy(out=a_sb[:, cols], in_=a_ps[n][:])

        nc.scalar.activation(gb[1][:], b_sb[:].indirect(l2[:, 16:32]), COPY)
        acc = sb.tile([P, J], F32)
        rej = sb.tile([P, J], F32)
        nc.vector.tensor_tensor(acc[:], a_sb[:].indirect(l1[:, 0:16]), gb[0][:], ALU.subtract)
        nc.scalar.activation(f1[:].indirect(l3[:]), acc[:], COPY)
        nc.vector.tensor_tensor(rej[:], a_sb[:].indirect(l1[:, 16:32]), gb[1][:], ALU.subtract)
        nc.scalar.activation(f2[:].indirect(l4[:]), rej[:], COPY)

        aa = sb.tile([P, T], F32)
        nc.vector.tensor_tensor(aa[:], a_sb[:], f1[:], ALU.add)
        gaa = sb.tile([P, I], F32)
        nc.scalar.activation(gaa[:], aa[:].indirect(l1[:]), COPY)
        bb = sb.tile([P, U], F32)
        for n in range(3):
            cols = slice(256 * n, 256 * (n + 1))
            nc.vector.tensor_tensor(bb[:, cols], b_ps[n][:], f2[:, cols], ALU.subtract)
        nc.gpsimd.tensor_tensor(bb[:, 768:U], b_sb[:, 768:U], f2[:, 768:U], ALU.subtract)
        gbb = sb.tile([P, I], F32)
        nc.vector.tensor_copy(gbb[:, 0:J], bb[:].indirect(l5[:, 0:16]))
        nc.scalar.activation(gbb[:, J:I], bb[:].indirect(l5[:, 16:32]), COPY)
        for h, queue in enumerate((nc.sync, nc.scalar)):
            cols = slice(J * h, J * (h + 1))
            res = sb.tile([P, J], F32, name="res%d" % h)
            nc.vector.tensor_tensor(res[:], gaa[:, cols], gbb[:, cols], ALU.max)
            queue.dma_start(out=out[:, cols], in_=res[:])
